import numpy as np
import ml_dtypes


def mxq(x, axis, fmt="e4m3"):
    dtype, down = {"e4m3": (ml_dtypes.float8_e4m3fn, 7), "e5m2": (ml_dtypes.float8_e5m2, 14)}[fmt]
    v = np.moveaxis(np.asarray(x, np.float32).astype(ml_dtypes.bfloat16).astype(np.float64), axis, -1)
    blocks = v.reshape(v.shape[:-1] + (-1, 32))
    amax = np.abs(blocks).max(-1, keepdims=True)
    byte = np.maximum(np.where(amax > 0, np.frexp(amax)[1] - 1 + 127, 0) - down, 1)
    scale = np.exp2(byte - 127.0)
    codes = (blocks / scale).astype(np.float32).astype(dtype).astype(np.float64)
    return np.moveaxis((codes * scale).reshape(v.shape), -1, axis)


WIDE = False


def mx_kscale(k):
    if not WIDE:
        return np.ones(k)
    levels = np.array([10, -10, 5, -5, 0])
    if k % 512:
        return np.exp2(np.random.permutation(np.resize(levels, k // 32))).repeat(32)
    a = np.empty((k // 512, 16))
    for p in range(k // 512):
        a[p, :8] = np.random.permutation(np.resize(levels, 8))
        for g in range(8):
            far = levels[np.abs(levels - a[p, g]) >= 10]
            a[p, g + 8] = far[np.random.randint(len(far))]
    return np.exp2(a.ravel()).repeat(32)


def f64(x):
    return np.asarray(x).astype(np.float64)


def striped(idx):
    return np.tile(idx.reshape(-1, 16).T, (8, 1)).astype(np.uint16)


def unstriped(offs):
    return offs[:16].T.reshape(-1).astype(np.int64)


E2M1 = np.array([0.0, 0.5, 1.0, 1.5, 2.0, 3.0, 4.0, 6.0, -0.0, -0.5, -1.0, -1.5, -2.0, -3.0, -4.0, -6.0])


def pack_fp4(w):
    k, n = w.shape
    w = f64(np.asarray(w, np.float32).astype(ml_dtypes.bfloat16)).reshape(k // 32, 32, n)
    amax = np.abs(w).max(1)
    mant, ex = np.frexp(amax / 6.0)
    byte = np.clip(np.where(amax > 0, np.where(mant > 0.5, ex, ex - 1) + 127, 1), 1, 254)
    scaled = (w * np.exp2(127.0 - byte)[:, None, :]).reshape(k, n).astype(np.float32)
    c = np.ascontiguousarray(scaled.reshape(k // 512, 128, 4, n).transpose(0, 1, 3, 2)).astype(ml_dtypes.float4_e2m1fn).view(np.uint8) & 0xF
    words = (c[..., 0::2] | (c[..., 1::2] << 4)).reshape(k // 512, 128, 2 * n)
    return np.ascontiguousarray(words), np.ascontiguousarray(byte.astype(np.uint8).reshape(k // 512, 16, n))


def unpack_fp4(words, scales):
    g, _, n = scales.shape
    words = np.ascontiguousarray(words).reshape(g, 128, n, 2)
    nib = np.empty((g, 128, n, 4), np.uint8)
    nib[..., 0::2] = words & 0xF
    nib[..., 1::2] = words >> 4
    vals = E2M1[nib] * np.repeat(np.exp2(scales.astype(np.float64) - 127.0), 8, axis=1)[..., None]
    return vals.transpose(0, 1, 3, 2).reshape(g * 512, n)


def relu(v):
    return np.maximum(v, 0.0)


K, T, S, V, N = 512, 2048, 768, 256, 128
P = 2 ** 7


def setup_inputs():
    n = np.random.standard_normal
    s = mx_kscale(K)[:, None]
    packed_w1 = pack_fp4(n((K, N)) / np.sqrt(K) / s)
    return {
        "xT": (n((K, T)) * s).astype(np.float32),
        "w1_words": packed_w1[0],
        "w1_scales": packed_w1[1],
        "margin": np.tile(np.random.uniform(0.2, 2.0, V), (P, 1)).astype(np.float32),
        "offs": striped(np.random.permutation(T)[:S]),
    }


def reference(xT, w1_words, w1_scales, margin, offs):
    xq = mxq(f64(xT)[:, unstriped(offs)], 0, "e4m3")
    h = unpack_fp4(w1_words, w1_scales).T @ xq
    near = (h[:, :V] - h[:, V:2 * V]) ** 2
    far = (h[:, :V] - h[:, 2 * V:3 * V]) ** 2
    return relu(near - far + f64(margin)[:1])

@@ -1,0 +1,99 @@
+import concourse.mybir as mybir
+
+F32 = mybir.dt.float32
+BF16 = mybir.dt.bfloat16
+I32 = mybir.dt.int32
+U32 = mybir.dt.uint32
+U16 = mybir.dt.uint16
+U8 = mybir.dt.uint8
+FP8X4 = mybir.dt.float8_e4m3fn_x4
+FP4X4 = mybir.dt.float4_e2m1fn_x4
+ALU = mybir.AluOpType
+ACT = mybir.ActivationFunctionType
+
+K, T, S, V, N = 512, 2048, 768, 256, 128
+P = 128
+PACK = 4
+FLOPS = 2 * K * N * S
+LAST_CHUNKS = (512, 512, 512, 512)
+HALF = V // 2
+
+
+def tile_picked_triplet_none_e_kernel(tc, xT, w1_words, w1_scales, margin, offs, out):
+    nc = tc.nc
+    with tc.tile_pool(name="sb", bufs=1) as sb, tc.psum_pool(name="ps", bufs=1) as ps:
+        rows = xT.rearrange("(p t) c -> t p c", t=PACK)
+        offsets = sb.tile([P, S // 16], U16, name="offsets")
+        planes = [sb.tile([P, T], F32, name="plane%d" % t) for t in range(PACK)]
+        plane3_bf = sb.tile([P, T], BF16, name="plane3_bf")
+        w_codes = sb.tile([P, 2 * N], U8, name="w_codes", align_bytes=64)
+        w_scales = sb.tile([P, N], U8, name="w_scales", align_bytes=64)
+        margins = sb.tile([P, V], F32, name="margins")
+        picked = sb.tile([P, S, PACK], BF16, name="picked", align_bytes=64)
+        staged = sb.tile([P, 2 * V], BF16, name="staged")
+
+        def entries(lo, hi):
+            return offsets[:, lo // 16 : hi // 16]
+
+        nc.vector.memset(w_scales[:].bitcast(I32), 0)
+        nc.sync.dma_start(planes[2][:], rows[2])
+        nc.sync.dma_start(offsets[:], offs)
+        nc.sync.dma_start(planes[0][:], rows[0])
+        nc.sync.dma_start(planes[1][:], rows[1])
+        c0 = 0
+        for width in LAST_CHUNKS:
+            nc.sync.dma_start(planes[3][:, c0 : c0 + width], rows[3][:, c0 : c0 + width])
+            c0 = c0 + width
+        nc.sync.dma_start(w_codes[:].bitcast(I32), w1_words[0].bitcast(I32))
+        for q in range(4):
+            nc.sync.dma_start(w_scales[32 * q : 32 * q + 4, :].bitcast(I32), w1_scales[0, 4 * q : 4 * q + 4, :].bitcast(I32))
+        nc.sync.dma_start(margins[:], margin)
+
+        nc.vector.tensor_copy(staged[:], planes[2][:].indirect(entries(V, S)))
+        nc.vector.tensor_copy(picked[:, 0:V, 2], planes[2][:].indirect(entries(0, V)))
+        nc.scalar.copy(picked[:, V:S, 2], staged[:])
+        nc.vector.tensor_copy(picked[:, :, 0], planes[0][:].indirect(offsets[:]))
+        nc.vector.tensor_copy(picked[:, :, 1], planes[1][:].indirect(offsets[:]))
+        c0 = 0
+        for width in LAST_CHUNKS:
+            nc.scalar.activation(plane3_bf[:, c0 : c0 + width], planes[3][:, c0 : c0 + width], ACT.Copy)
+            c0 = c0 + width
+        nc.vector.tensor_copy(picked[:, 0:V, 3], planes[3][:].indirect(entries(0, V)))
+        nc.scalar.activation(picked[:, V : 2 * V, 3], plane3_bf[:].indirect(entries(V, 2 * V)), ACT.Copy)
+        nc.scalar.activation(picked[:, 2 * V : S, 3], plane3_bf[:].indirect(entries(2 * V, S)), ACT.Copy)
+
+        def project(name, lo, hi):
+            codes = sb.tile([P, hi - lo], U32, name="codes_" + name, align_bytes=64)
+            scales = sb.tile([P, hi - lo], U8, name="scales_" + name, align_bytes=64)
+            h = ps.tile([P, hi - lo], F32, name="h_" + name)
+            nc.vector.quantize_mx(codes[:].bitcast(FP8X4), scales[:], picked[:, lo:hi, :].rearrange("p n t -> p (n t)"))
+            nc.tensor.matmul_mx(h[:], lhsT=w_codes[:].bitcast(FP4X4), lhsT_scale=w_scales[:],
+                                rhs=codes[:].bitcast(FP8X4), rhs_scale=scales[:], start=True, stop=True)
+            return h
+
+        h_anchor = project("anchor", 0, V)
+        h_pos = project("pos", V, 2 * V)
+        h_neg = [project("neg%d" % j, 2 * V + j * HALF, 2 * V + (j + 1) * HALF) for j in range(2)]
+
+        anchor = sb.tile([P, V], F32, name="anchor")
+        d_pos = sb.tile([P, V], F32, name="d_pos")
+        near = sb.tile([P, V], F32, name="near")
+        near_m = sb.tile([P, V], F32, name="near_m")
+        nc.scalar.copy(anchor[:], h_anchor[:])
+        nc.vector.tensor_tensor(d_pos[:], h_pos[:], anchor[:], ALU.subtract)
+        nc.scalar.activation(near[:], d_pos[:], ACT.Square)
+        halves = [slice(j * HALF, (j + 1) * HALF) for j in range(2)]
+        d_neg = [sb.tile([P, HALF], F32, name="d_neg%d" % j) for j in range(2)]
+        far = [sb.tile([P, HALF], F32, name="far%d" % j) for j in range(2)]
+        gap = [sb.tile([P, HALF], F32, name="gap%d" % j) for j in range(2)]
+        loss = [sb.tile([P, HALF], F32, name="loss%d" % j) for j in range(2)]
+        for j in range(2):
+            nc.vector.tensor_tensor(d_neg[j][:], h_neg[j][:], anchor[:, halves[j]], ALU.subtract)
+        for j in range(2):
+            nc.scalar.activation(far[j][:], d_neg[j][:], ACT.Square)
+        nc.vector.tensor_tensor(near_m[:], near[:], margins[:], ALU.add)
+        for j in range(2):
+            nc.vector.tensor_tensor(gap[j][:], near_m[:, halves[j]], far[j][:], ALU.subtract)
+        for j in range(2):
+            nc.scalar.activation(loss[j][:], gap[j][:], ACT.Relu)
+            nc.sync.dma_start(out[:, halves[j]], loss[j][:])

@@ -1,4 +1,5 @@
 import concourse.mybir as mybir
+from concourse.masks import make_identity
 
 F32 = mybir.dt.float32
 BF16 = mybir.dt.bfloat16
@@ -15,7 +16,7 @@ K, T, S, V, N = 512, 2048, 768, 256, 128
 P = 128
 PACK = 4
 FLOPS = 2 * K * N * S
-LAST_CHUNKS = (512, 512, 512, 512)
+CHUNKS = {0: (2048,), 2: (1024, 1024), 1: (2048,), 3: (768, 768, 512)}
 HALF = V // 2
 
 
@@ -25,75 +26,83 @@ def tile_picked_triplet_none_e_kernel(tc, xT, w1_words, w1_scales, margin, offs,
         rows = xT.rearrange("(p t) c -> t p c", t=PACK)
         offsets = sb.tile([P, S // 16], U16, name="offsets")
         planes = [sb.tile([P, T], F32, name="plane%d" % t) for t in range(PACK)]
-        plane3_bf = sb.tile([P, T], BF16, name="plane3_bf")
+        rounded = {t: sb.tile([P, T], BF16, name="rounded%d" % t) for t in (2, 3)}
         w_codes = sb.tile([P, 2 * N], U8, name="w_codes", align_bytes=64)
         w_scales = sb.tile([P, N], U8, name="w_scales", align_bytes=64)
-        margins = sb.tile([P, V], F32, name="margins")
+        margins = sb.tile([P, 2], F32, name="margins")
+        ident = sb.tile([P, P], F32, name="ident")
         picked = sb.tile([P, S, PACK], BF16, name="picked", align_bytes=64)
-        staged = sb.tile([P, 2 * V], BF16, name="staged")
 
         def entries(lo, hi):
             return offsets[:, lo // 16 : hi // 16]
 
+        def chunks(t):
+            starts = [sum(CHUNKS[t][:i]) for i in range(len(CHUNKS[t]) + 1)]
+            return [slice(a, b) for a, b in zip(starts, starts[1:])]
+
         nc.vector.memset(w_scales[:].bitcast(I32), 0)
-        nc.sync.dma_start(planes[2][:], rows[2])
-        nc.sync.dma_start(offsets[:], offs)
-        nc.sync.dma_start(planes[0][:], rows[0])
-        nc.sync.dma_start(planes[1][:], rows[1])
-        c0 = 0
-        for width in LAST_CHUNKS:
-            nc.sync.dma_start(planes[3][:, c0 : c0 + width], rows[3][:, c0 : c0 + width])
-            c0 = c0 + width
+        make_identity(nc, ident[:])
+        for t in CHUNKS:
+            for cols in chunks(t):
+                nc.sync.dma_start(planes[t][:, cols], rows[t][:, cols])
+            if t == 0:
+                nc.sync.dma_start(offsets[:], offs)
         nc.sync.dma_start(w_codes[:].bitcast(I32), w1_words[0].bitcast(I32))
         for q in range(4):
             nc.sync.dma_start(w_scales[32 * q : 32 * q + 4, :].bitcast(I32), w1_scales[0, 4 * q : 4 * q + 4, :].bitcast(I32))
-        nc.sync.dma_start(margins[:], margin)
+        with nc.allow_non_contiguous_dma(reason="one margin a partition"):
+            nc.sync.dma_start(margins[:], margin[0].rearrange("(j p) -> p j", p=P))
 
-        nc.vector.tensor_copy(staged[:], planes[2][:].indirect(entries(V, S)))
-        nc.vector.tensor_copy(picked[:, 0:V, 2], planes[2][:].indirect(entries(0, V)))
-        nc.scalar.copy(picked[:, V:S, 2], staged[:])
-        nc.vector.tensor_copy(picked[:, :, 0], planes[0][:].indirect(offsets[:]))
-        nc.vector.tensor_copy(picked[:, :, 1], planes[1][:].indirect(offsets[:]))
-        c0 = 0
-        for width in LAST_CHUNKS:
-            nc.scalar.activation(plane3_bf[:, c0 : c0 + width], planes[3][:, c0 : c0 + width], ACT.Copy)
-            c0 = c0 + width
-        nc.vector.tensor_copy(picked[:, 0:V, 3], planes[3][:].indirect(entries(0, V)))
-        nc.scalar.activation(picked[:, V : 2 * V, 3], plane3_bf[:].indirect(entries(V, 2 * V)), ACT.Copy)
-        nc.scalar.activation(picked[:, 2 * V : S, 3], plane3_bf[:].indirect(entries(2 * V, S)), ACT.Copy)
+        def by_vector(t, lo, hi):
+            nc.vector.tensor_copy(picked[:, lo:hi, t], planes[t][:].indirect(entries(lo, hi)))
 
-        def project(name, lo, hi):
-            codes = sb.tile([P, hi - lo], U32, name="codes_" + name, align_bytes=64)
-            scales = sb.tile([P, hi - lo], U8, name="scales_" + name, align_bytes=64)
-            h = ps.tile([P, hi - lo], F32, name="h_" + name)
-            nc.vector.quantize_mx(codes[:].bitcast(FP8X4), scales[:], picked[:, lo:hi, :].rearrange("p n t -> p (n t)"))
-            nc.tensor.matmul_mx(h[:], lhsT=w_codes[:].bitcast(FP4X4), lhsT_scale=w_scales[:],
-                                rhs=codes[:].bitcast(FP8X4), rhs_scale=scales[:], start=True, stop=True)
-            return h
+        def by_scalar(t, lo, hi):
+            for cols in chunks(t):
+                nc.scalar.activation(rounded[t][:, cols], planes[t][:, cols], ACT.Copy)
+            nc.scalar.activation(picked[:, lo:hi, t], rounded[t][:].indirect(entries(lo, hi)), ACT.Copy)
 
-        h_anchor = project("anchor", 0, V)
-        h_pos = project("pos", V, 2 * V)
-        h_neg = [project("neg%d" % j, 2 * V + j * HALF, 2 * V + (j + 1) * HALF) for j in range(2)]
+        by_vector(0, 0, S)
+        by_vector(2, 0, 2 * V)
+        by_scalar(2, 2 * V, S)
+        by_vector(1, 0, S)
+        by_vector(3, 0, V)
+        by_vector(3, V, 2 * V)
+        by_scalar(3, 2 * V, S)
 
-        anchor = sb.tile([P, V], F32, name="anchor")
-        d_pos = sb.tile([P, V], F32, name="d_pos")
-        near = sb.tile([P, V], F32, name="near")
-        near_m = sb.tile([P, V], F32, name="near_m")
-        nc.scalar.copy(anchor[:], h_anchor[:])
-        nc.vector.tensor_tensor(d_pos[:], h_pos[:], anchor[:], ALU.subtract)
-        nc.scalar.activation(near[:], d_pos[:], ACT.Square)
-        halves = [slice(j * HALF, (j + 1) * HALF) for j in range(2)]
-        d_neg = [sb.tile([P, HALF], F32, name="d_neg%d" % j) for j in range(2)]
-        far = [sb.tile([P, HALF], F32, name="far%d" % j) for j in range(2)]
-        gap = [sb.tile([P, HALF], F32, name="gap%d" % j) for j in range(2)]
+        def project(name, lo, h):
+            codes = sb.tile([P, HALF], U32, name="codes_" + name, align_bytes=64)
+            scales = sb.tile([P, HALF], U8, name="scales_" + name, align_bytes=64)
+            nc.vector.quantize_mx(codes[:].bitcast(FP8X4), scales[:], picked[:, lo : lo + HALF, :].rearrange("p n t -> p (n t)"))
+            nc.tensor.matmul_mx(h, lhsT=codes[:].bitcast(FP8X4), lhsT_scale=scales[:],
+                                rhs=w_codes[:].bitcast(FP4X4), rhs_scale=w_scales[:], start=True, stop=True)
+
+        h_anchor = [ps.tile([P, N], F32, name="h_anchor%d" % j) for j in range(2)]
+        h_other = [ps.tile([P, 2, N], F32, name="h_other%d" % j) for j in range(2)]
+        gap = [ps.tile([P, HALF], F32, name="gap%d" % j) for j in range(2)]
+        project("anchor0", 0, h_anchor[0][:])
+        project("pos0", V, h_other[0][:, 0, :])
+        project("anchor1", HALF, h_anchor[1][:])
+        project("neg0", 2 * V, h_other[0][:, 1, :])
+        project("pos1", V + HALF, h_other[1][:, 0, :])
+        project("neg1", 2 * V + HALF, h_other[1][:, 1, :])
+
+        anchor = [sb.tile([P, N], F32, name="anchor%d" % j) for j in range(2)]
+        diff = [sb.tile([P, 2, N], F32, name="diff%d" % j) for j in range(2)]
+        near = [sb.tile([P, N], F32, name="near%d" % j) for j in range(2)]
+        far_neg = [sb.tile([P, N], F32, name="far_neg%d" % j) for j in range(2)]
         loss = [sb.tile([P, HALF], F32, name="loss%d" % j) for j in range(2)]
         for j in range(2):
-            nc.vector.tensor_tensor(d_neg[j][:], h_neg[j][:], anchor[:, halves[j]], ALU.subtract)
+            nc.scalar.copy(anchor[j][:], h_anchor[j][:])
         for j in range(2):
-            nc.scalar.activation(far[j][:], d_neg[j][:], ACT.Square)
-        nc.vector.tensor_tensor(near_m[:], near[:], margins[:], ALU.add)
+            nc.vector.tensor_tensor(diff[j][:], h_other[j][:], anchor[j][:].unsqueeze(1).broadcast_to([P, 2, N]), ALU.subtract)
         for j in range(2):
-            nc.vector.tensor_tensor(gap[j][:], near_m[:, halves[j]], far[j][:], ALU.subtract)
+            nc.scalar.activation(near[j][:], diff[j][:, 0, :], ACT.Square)
+            nc.vector.scalar_tensor_tensor(far_neg[j][:], diff[j][:, 1, :], -1.0, diff[j][:, 1, :], ALU.mult, ALU.mult)
         for j in range(2):
-            nc.scalar.activation(loss[j][:], gap[j][:], ACT.Relu)
-            nc.sync.dma_start(out[:, halves[j]], loss[j][:])
+            nc.tensor.matmul(gap[j][:], lhsT=margins[:, j : j + 1].to_broadcast([P, N]), rhs=ident[:], start=True, stop=False, is_transpose=True)
+            nc.tensor.matmul(gap[j][:], lhsT=near[j][:], rhs=ident[:], start=False, stop=False, is_transpose=True)
+            nc.tensor.matmul(gap[j][:], lhsT=far_neg[j][:], rhs=ident[:], start=False, stop=True, is_transpose=True)
+        nc.scalar.activation(loss[0][:], gap[0][:], ACT.Relu)
+        nc.vector.tensor_scalar_max(loss[1][:], gap[1][:], 0.0)
+        for j in range(2):
+            nc.sync.dma_start(out[:, j * HALF : (j + 1) * HALF], loss[j][:])

@@ -30,6 +30,7 @@ def tile_picked_triplet_none_e_kernel(tc, xT, w1_words, w1_scales, margin, offs,
         w_codes = sb.tile([P, 2 * N], U8, name="w_codes", align_bytes=64)
         w_scales = sb.tile([P, N], U8, name="w_scales", align_bytes=64)
         margins = sb.tile([P, 2], F32, name="margins")
+        margin_row = sb.tile([P, V], F32, name="margin_row")
         ident = sb.tile([P, P], F32, name="ident")
         picked = sb.tile([P, S, PACK], BF16, name="picked", align_bytes=64)
 
@@ -41,17 +42,25 @@ def tile_picked_triplet_none_e_kernel(tc, xT, w1_words, w1_scales, margin, offs,
             return [slice(a, b) for a, b in zip(starts, starts[1:])]
 
         nc.vector.memset(w_scales[:].bitcast(I32), 0)
+        nc.vector.memset(margin_row[:], 0.0)
         make_identity(nc, ident[:])
         for t in CHUNKS:
             for cols in chunks(t):
                 nc.sync.dma_start(planes[t][:, cols], rows[t][:, cols])
             if t == 0:
                 nc.sync.dma_start(offsets[:], offs)
+                nc.sync.dma_start(margin_row[0:1, :], margin[0:1, :])
         nc.sync.dma_start(w_codes[:].bitcast(I32), w1_words[0].bitcast(I32))
         for q in range(4):
             nc.sync.dma_start(w_scales[32 * q : 32 * q + 4, :].bitcast(I32), w1_scales[0, 4 * q : 4 * q + 4, :].bitcast(I32))
-        with nc.allow_non_contiguous_dma(reason="one margin a partition"):
-            nc.sync.dma_start(margins[:], margin[0].rearrange("(j p) -> p j", p=P))
+
+        gap = [ps.tile([P, HALF], F32, name="gap%d" % j) for j in range(2)]
+        turned = ps.tile([P, 2, P], F32, name="turned", tag="h_anchor0")
+        for j in range(2):
+            nc.tensor.transpose(turned[:, j, :], margin_row[:, j * HALF : (j + 1) * HALF], ident[:])
+        nc.scalar.copy(margins[:], turned[:, :, 0])
+        for j in range(2):
+            nc.tensor.matmul(gap[j][:], lhsT=margins[:, j : j + 1].to_broadcast([P, N]), rhs=ident[:], start=True, stop=False, is_transpose=True)
 
         def by_vector(t, lo, hi):
             nc.vector.tensor_copy(picked[:, lo:hi, t], planes[t][:].indirect(entries(lo, hi)))
@@ -76,30 +85,30 @@ def tile_picked_triplet_none_e_kernel(tc, xT, w1_words, w1_scales, margin, offs,
             nc.tensor.matmul_mx(h, lhsT=codes[:].bitcast(FP8X4), lhsT_scale=scales[:],
                                 rhs=w_codes[:].bitcast(FP4X4), rhs_scale=w_scales[:], start=True, stop=True)
 
-        h_anchor = [ps.tile([P, N], F32, name="h_anchor%d" % j) for j in range(2)]
-        h_other = [ps.tile([P, 2, N], F32, name="h_other%d" % j) for j in range(2)]
-        gap = [ps.tile([P, HALF], F32, name="gap%d" % j) for j in range(2)]
-        project("anchor0", 0, h_anchor[0][:])
-        project("pos0", V, h_other[0][:, 0, :])
-        project("anchor1", HALF, h_anchor[1][:])
-        project("neg0", 2 * V, h_other[0][:, 1, :])
-        project("pos1", V + HALF, h_other[1][:, 0, :])
-        project("neg1", 2 * V + HALF, h_other[1][:, 1, :])
+        h_anchor = [ps.tile([P, N], F32, name="h_anchor%d" % j, tag="h_anchor%d" % j) for j in range(2)]
+        h_pos = [ps.tile([P, N], F32, name="h_pos%d" % j) for j in range(2)]
+        h_neg = [ps.tile([P, N], F32, name="h_neg%d" % j) for j in range(2)]
+        for j in range(2):
+            project("anchor%d" % j, j * HALF, h_anchor[j][:])
+        for j in range(2):
+            project("pos%d" % j, V + j * HALF, h_pos[j][:])
+        for j in range(2):
+            project("neg%d" % j, 2 * V + j * HALF, h_neg[j][:])
 
-        anchor = [sb.tile([P, N], F32, name="anchor%d" % j) for j in range(2)]
-        diff = [sb.tile([P, 2, N], F32, name="diff%d" % j) for j in range(2)]
-        near = [sb.tile([P, N], F32, name="near%d" % j) for j in range(2)]
-        far_neg = [sb.tile([P, N], F32, name="far_neg%d" % j) for j in range(2)]
-        loss = [sb.tile([P, HALF], F32, name="loss%d" % j) for j in range(2)]
+        def pair(name):
+            return [sb.tile([P, N], F32, name="%s%d" % (name, j)) for j in range(2)]
+
+        anchor, d_pos, d_neg, near, far_neg, loss = [pair(name) for name in ("anchor", "d_pos", "d_neg", "near", "far_neg", "loss")]
         for j in range(2):
             nc.scalar.copy(anchor[j][:], h_anchor[j][:])
         for j in range(2):
-            nc.vector.tensor_tensor(diff[j][:], h_other[j][:], anchor[j][:].unsqueeze(1).broadcast_to([P, 2, N]), ALU.subtract)
+            nc.vector.tensor_tensor(d_pos[j][:], h_pos[j][:], anchor[j][:], ALU.subtract)
         for j in range(2):
-            nc.scalar.activation(near[j][:], diff[j][:, 0, :], ACT.Square)
-            nc.vector.scalar_tensor_tensor(far_neg[j][:], diff[j][:, 1, :], -1.0, diff[j][:, 1, :], ALU.mult, ALU.mult)
+            nc.vector.tensor_tensor(d_neg[j][:], h_neg[j][:], anchor[j][:], ALU.subtract)
         for j in range(2):
-            nc.tensor.matmul(gap[j][:], lhsT=margins[:, j : j + 1].to_broadcast([P, N]), rhs=ident[:], start=True, stop=False, is_transpose=True)
+            nc.scalar.activation(near[j][:], d_pos[j][:], ACT.Square)
+            nc.vector.scalar_tensor_tensor(far_neg[j][:], d_neg[j][:], -1.0, d_neg[j][:], ALU.mult, ALU.mult)
+        for j in range(2):
             nc.tensor.matmul(gap[j][:], lhsT=near[j][:], rhs=ident[:], start=False, stop=False, is_transpose=True)
             nc.tensor.matmul(gap[j][:], lhsT=far_neg[j][:], rhs=ident[:], start=False, stop=True, is_transpose=True)
         nc.scalar.activation(loss[0][:], gap[0][:], ACT.Relu)

@@ -1,5 +1,4 @@
 import concourse.mybir as mybir
-from concourse.masks import make_identity
 
 F32 = mybir.dt.float32
 BF16 = mybir.dt.bfloat16
@@ -16,7 +15,6 @@ K, T, S, V, N = 512, 2048, 768, 256, 128
 P = 128
 PACK = 4
 FLOPS = 2 * K * N * S
-CHUNKS = {0: (2048,), 2: (1024, 1024), 1: (2048,), 3: (768, 768, 512)}
 HALF = V // 2
 
 
@@ -26,92 +24,85 @@ def tile_picked_triplet_none_e_kernel(tc, xT, w1_words, w1_scales, margin, offs,
         rows = xT.rearrange("(p t) c -> t p c", t=PACK)
         offsets = sb.tile([P, S // 16], U16, name="offsets")
         planes = [sb.tile([P, T], F32, name="plane%d" % t) for t in range(PACK)]
-        rounded = {t: sb.tile([P, T], BF16, name="rounded%d" % t) for t in (2, 3)}
         w_codes = sb.tile([P, 2 * N], U8, name="w_codes", align_bytes=64)
         w_scales = sb.tile([P, N], U8, name="w_scales", align_bytes=64)
-        margins = sb.tile([P, 2], F32, name="margins")
-        margin_row = sb.tile([P, V], F32, name="margin_row")
-        ident = sb.tile([P, P], F32, name="ident")
-        picked = sb.tile([P, S, PACK], BF16, name="picked", align_bytes=64)
+        margins = sb.tile([P, V], F32, name="margins")
 
-        def entries(lo, hi):
-            return offsets[:, lo // 16 : hi // 16]
-
-        def chunks(t):
-            starts = [sum(CHUNKS[t][:i]) for i in range(len(CHUNKS[t]) + 1)]
-            return [slice(a, b) for a, b in zip(starts, starts[1:])]
+        def entries(lo, n):
+            return offsets[:, lo // 16 : (lo + n) // 16]
 
         nc.vector.memset(w_scales[:].bitcast(I32), 0)
-        nc.vector.memset(margin_row[:], 0.0)
-        make_identity(nc, ident[:])
-        for t in CHUNKS:
-            for cols in chunks(t):
-                nc.sync.dma_start(planes[t][:, cols], rows[t][:, cols])
+        for t in range(PACK):
+            nc.sync.dma_start(planes[t][:], rows[t])
             if t == 0:
                 nc.sync.dma_start(offsets[:], offs)
-                nc.sync.dma_start(margin_row[0:1, :], margin[0:1, :])
         nc.sync.dma_start(w_codes[:].bitcast(I32), w1_words[0].bitcast(I32))
         for q in range(4):
             nc.sync.dma_start(w_scales[32 * q : 32 * q + 4, :].bitcast(I32), w1_scales[0, 4 * q : 4 * q + 4, :].bitcast(I32))
+        nc.sync.dma_start(margins[:], margin)
 
-        gap = [ps.tile([P, HALF], F32, name="gap%d" % j) for j in range(2)]
-        turned = ps.tile([P, 2, P], F32, name="turned", tag="h_anchor0")
-        for j in range(2):
-            nc.tensor.transpose(turned[:, j, :], margin_row[:, j * HALF : (j + 1) * HALF], ident[:])
-        nc.scalar.copy(margins[:], turned[:, :, 0])
-        for j in range(2):
-            nc.tensor.matmul(gap[j][:], lhsT=margins[:, j : j + 1].to_broadcast([P, N]), rhs=ident[:], start=True, stop=False, is_transpose=True)
+        pieces = {"p0": V, "n0": 2 * V, "p1": V + HALF, "n1": 2 * V + HALF}
+        picked_a = sb.tile([P, V, PACK], BF16, name="picked_a", align_bytes=64)
+        picked = {k: sb.tile([P, HALF, PACK], BF16, name="picked_" + k, align_bytes=64) for k in pieces}
+        dense = {(k, u): sb.tile([P, 2, HALF], BF16, name="dense_%s_%d" % (k, u)) for k in pieces for u in range(2)}
 
-        def by_vector(t, lo, hi):
-            nc.vector.tensor_copy(picked[:, lo:hi, t], planes[t][:].indirect(entries(lo, hi)))
+        def place(k, u):
+            nc.vector.tensor_copy(picked[k][:, :, 2 * u : 2 * u + 2], dense[k, u][:].rearrange("p t n -> p n t"))
 
-        def by_scalar(t, lo, hi):
-            for cols in chunks(t):
-                nc.scalar.activation(rounded[t][:, cols], planes[t][:, cols], ACT.Copy)
-            nc.scalar.activation(picked[:, lo:hi, t], rounded[t][:].indirect(entries(lo, hi)), ACT.Copy)
+        def quantize(name, source, n):
+            codes = sb.tile([P, n], U32, name="codes_" + name, align_bytes=64)
+            scales = sb.tile([P, n], U8, name="scales_" + name, align_bytes=64)
+            nc.vector.quantize_mx(codes[:].bitcast(FP8X4), scales[:], source.rearrange("p n t -> p (n t)"))
+            return codes, scales
 
-        by_vector(0, 0, S)
-        by_vector(2, 0, 2 * V)
-        by_scalar(2, 2 * V, S)
-        by_vector(1, 0, S)
-        by_vector(3, 0, V)
-        by_vector(3, V, 2 * V)
-        by_scalar(3, 2 * V, S)
+        def project(h, operand, start, stop):
+            codes, scales = operand
+            nc.tensor.matmul_mx(h[:], lhsT=w_codes[:].bitcast(FP4X4), lhsT_scale=w_scales[:],
+                                rhs=codes[:].bitcast(FP8X4), rhs_scale=scales[:], start=start, stop=stop)
 
-        def project(name, lo, h):
-            codes = sb.tile([P, HALF], U32, name="codes_" + name, align_bytes=64)
-            scales = sb.tile([P, HALF], U8, name="scales_" + name, align_bytes=64)
-            nc.vector.quantize_mx(codes[:].bitcast(FP8X4), scales[:], picked[:, lo : lo + HALF, :].rearrange("p n t -> p (n t)"))
-            nc.tensor.matmul_mx(h, lhsT=codes[:].bitcast(FP8X4), lhsT_scale=scales[:],
-                                rhs=w_codes[:].bitcast(FP4X4), rhs_scale=w_scales[:], start=True, stop=True)
+        for t in range(PACK):
+            nc.vector.tensor_copy(picked_a[:, :, t], planes[t][:].indirect(entries(0, V)))
+            for k, lo in pieces.items():
+                nc.scalar.activation(dense[k, t // 2][:, t % 2, :], planes[t][:].indirect(entries(lo, HALF)), ACT.Copy, scale=-1.0)
+            if t == 1:
+                for k in pieces:
+                    place(k, 0)
 
-        h_anchor = [ps.tile([P, N], F32, name="h_anchor%d" % j, tag="h_anchor%d" % j) for j in range(2)]
-        h_pos = [ps.tile([P, N], F32, name="h_pos%d" % j) for j in range(2)]
-        h_neg = [ps.tile([P, N], F32, name="h_neg%d" % j) for j in range(2)]
-        for j in range(2):
-            project("anchor%d" % j, j * HALF, h_anchor[j][:])
-        for j in range(2):
-            project("pos%d" % j, V + j * HALF, h_pos[j][:])
-        for j in range(2):
-            project("neg%d" % j, 2 * V + j * HALF, h_neg[j][:])
+        x0, y0, z0, g1, g2 = [ps.tile([P, HALF], F32, name=name) for name in ("x0", "y0", "z0", "g1", "g2")]
+        anchor0, d_pos0, far0 = [sb.tile([P, HALF], F32, name=name) for name in ("anchor0", "d_pos0", "far0")]
+        d_neg0 = sb.tile([P, HALF], F32, name="d_neg0", tag="neg")
+        near, near_m, gap, loss = [[sb.tile([P, HALF], F32, name="%s%d" % (name, j)) for j in range(2)]
+                                   for name in ("near", "near_m", "gap", "loss")]
 
-        def pair(name):
-            return [sb.tile([P, N], F32, name="%s%d" % (name, j)) for j in range(2)]
+        def cols(j):
+            return slice(j * HALF, (j + 1) * HALF)
 
-        anchor, d_pos, d_neg, near, far_neg, loss = [pair(name) for name in ("anchor", "d_pos", "d_neg", "near", "far_neg", "loss")]
-        for j in range(2):
-            nc.scalar.copy(anchor[j][:], h_anchor[j][:])
-        for j in range(2):
-            nc.vector.tensor_tensor(d_pos[j][:], h_pos[j][:], anchor[j][:], ALU.subtract)
-        for j in range(2):
-            nc.vector.tensor_tensor(d_neg[j][:], h_neg[j][:], anchor[j][:], ALU.subtract)
-        for j in range(2):
-            nc.scalar.activation(near[j][:], d_pos[j][:], ACT.Square)
-            nc.vector.scalar_tensor_tensor(far_neg[j][:], d_neg[j][:], -1.0, d_neg[j][:], ALU.mult, ALU.mult)
-        for j in range(2):
-            nc.tensor.matmul(gap[j][:], lhsT=near[j][:], rhs=ident[:], start=False, stop=False, is_transpose=True)
-            nc.tensor.matmul(gap[j][:], lhsT=far_neg[j][:], rhs=ident[:], start=False, stop=True, is_transpose=True)
-        nc.scalar.activation(loss[0][:], gap[0][:], ACT.Relu)
-        nc.vector.tensor_scalar_max(loss[1][:], gap[1][:], 0.0)
-        for j in range(2):
-            nc.sync.dma_start(out[:, j * HALF : (j + 1) * HALF], loss[j][:])
+        place("p0", 1)
+        qa0 = quantize("a0", picked_a[:, cols(0), :], HALF)
+        project(x0, qa0, True, True)
+        nc.scalar.copy(anchor0[:], x0[:])
+        place("n0", 1)
+        project(y0, quantize("p0", picked["p0"][:], HALF), True, True)
+        place("p1", 1)
+        project(z0, quantize("n0", picked["n0"][:], HALF), True, True)
+        qa1 = quantize("a1", picked_a[:, cols(1), :], HALF)
+        project(g1, qa1, True, False)
+        project(g2, qa1, True, False)
+        project(g1, quantize("p1", picked["p1"][:], HALF), False, True)
+        place("n1", 1)
+        nc.vector.tensor_tensor(d_pos0[:], y0[:], anchor0[:], ALU.add)
+        project(g2, quantize("n1", picked["n1"][:], HALF), False, True)
+        nc.vector.tensor_tensor(d_neg0[:], z0[:], anchor0[:], ALU.add)
+
+        nc.scalar.activation(near[1][:], g1[:], ACT.Square)
+        nc.scalar.activation(near[0][:], d_pos0[:], ACT.Square)
+        nc.scalar.activation(far0[:], d_neg0[:], ACT.Square)
+        far = [far0, sb.tile([P, HALF], F32, name="far1", tag="neg")]
+        nc.scalar.activation(far[1][:], g2[:], ACT.Square)
+        for j in (1, 0):
+            nc.vector.tensor_tensor(near_m[j][:], near[j][:], margins[:, cols(j)], ALU.add)
+        for j in (0, 1):
+            nc.vector.tensor_tensor(gap[j][:], near_m[j][:], far[j][:], ALU.subtract)
+        for j in (0, 1):
+            nc.vector.tensor_scalar_max(loss[j][:], gap[j][:], 0.0)
+            nc.sync.dma_start(out[:, cols(j)], loss[j][:])

@@ -46,8 +46,8 @@ def tile_picked_triplet_none_e_kernel(tc, xT, w1_words, w1_scales, margin, offs,
         picked = {k: sb.tile([P, HALF, PACK], BF16, name="picked_" + k, align_bytes=64) for k in pieces}
         dense = {(k, u): sb.tile([P, 2, HALF], BF16, name="dense_%s_%d" % (k, u)) for k in pieces for u in range(2)}
 
-        def place(k, u):
-            nc.vector.tensor_copy(picked[k][:, :, 2 * u : 2 * u + 2], dense[k, u][:].rearrange("p t n -> p n t"))
+        def place(k, u, copy=nc.vector.tensor_copy):
+            copy(picked[k][:, :, 2 * u : 2 * u + 2], dense[k, u][:].rearrange("p t n -> p n t"))
 
         def quantize(name, source, n):
             codes = sb.tile([P, n], U32, name="codes_" + name, align_bytes=64)
@@ -69,37 +69,37 @@ def tile_picked_triplet_none_e_kernel(tc, xT, w1_words, w1_scales, margin, offs,
                     place(k, 0)
 
         x0, y0, z0, g1, g2 = [ps.tile([P, HALF], F32, name=name) for name in ("x0", "y0", "z0", "g1", "g2")]
-        anchor0, d_pos0, far0 = [sb.tile([P, HALF], F32, name=name) for name in ("anchor0", "d_pos0", "far0")]
-        d_neg0 = sb.tile([P, HALF], F32, name="d_neg0", tag="neg")
+        d_pos0, d_neg0, far0 = [sb.tile([P, HALF], F32, name=name) for name in ("d_pos0", "d_neg0", "far0")]
+        anchor0 = sb.tile([P, HALF], F32, name="anchor0", tag="anchor0")
         near, near_m, gap, loss = [[sb.tile([P, HALF], F32, name="%s%d" % (name, j)) for j in range(2)]
                                    for name in ("near", "near_m", "gap", "loss")]
 
         def cols(j):
             return slice(j * HALF, (j + 1) * HALF)
 
+        place("p1", 1, nc.scalar.copy)
+        place("n1", 1, nc.scalar.copy)
         place("p0", 1)
         qa0 = quantize("a0", picked_a[:, cols(0), :], HALF)
         project(x0, qa0, True, True)
         nc.scalar.copy(anchor0[:], x0[:])
         place("n0", 1)
         project(y0, quantize("p0", picked["p0"][:], HALF), True, True)
-        place("p1", 1)
-        project(z0, quantize("n0", picked["n0"][:], HALF), True, True)
         qa1 = quantize("a1", picked_a[:, cols(1), :], HALF)
+        project(z0, quantize("n0", picked["n0"][:], HALF), True, True)
         project(g1, qa1, True, False)
         project(g2, qa1, True, False)
         project(g1, quantize("p1", picked["p1"][:], HALF), False, True)
-        place("n1", 1)
-        nc.vector.tensor_tensor(d_pos0[:], y0[:], anchor0[:], ALU.add)
         project(g2, quantize("n1", picked["n1"][:], HALF), False, True)
+        nc.vector.tensor_tensor(d_pos0[:], y0[:], anchor0[:], ALU.add)
         nc.vector.tensor_tensor(d_neg0[:], z0[:], anchor0[:], ALU.add)
 
-        nc.scalar.activation(near[1][:], g1[:], ACT.Square)
         nc.scalar.activation(near[0][:], d_pos0[:], ACT.Square)
+        nc.scalar.activation(near[1][:], g1[:], ACT.Square)
         nc.scalar.activation(far0[:], d_neg0[:], ACT.Square)
-        far = [far0, sb.tile([P, HALF], F32, name="far1", tag="neg")]
+        far = [far0, sb.tile([P, HALF], F32, name="far1", tag="anchor0")]
         nc.scalar.activation(far[1][:], g2[:], ACT.Square)
-        for j in (1, 0):
+        for j in (0, 1):
             nc.vector.tensor_tensor(near_m[j][:], near[j][:], margins[:, cols(j)], ALU.add)
         for j in (0, 1):
             nc.vector.tensor_tensor(gap[j][:], near_m[j][:], far[j][:], ALU.subtract)

@@ -41,8 +41,8 @@ def tile_picked_triplet_none_e_kernel(tc, xT, w1_words, w1_scales, margin, offs,
             nc.sync.dma_start(w_scales[32 * q : 32 * q + 4, :].bitcast(I32), w1_scales[0, 4 * q : 4 * q + 4, :].bitcast(I32))
         nc.sync.dma_start(margins[:], margin)
 
-        pieces = {"p0": V, "n0": 2 * V, "p1": V + HALF, "n1": 2 * V + HALF}
-        picked_a = sb.tile([P, V, PACK], BF16, name="picked_a", align_bytes=64)
+        pieces = {"n0": 2 * V, "p1": V + HALF, "n1": 2 * V + HALF}
+        picked_a = sb.tile([P, V + HALF, PACK], BF16, name="picked_a", align_bytes=64)
         picked = {k: sb.tile([P, HALF, PACK], BF16, name="picked_" + k, align_bytes=64) for k in pieces}
         dense = {(k, u): sb.tile([P, 2, HALF], BF16, name="dense_%s_%d" % (k, u)) for k in pieces for u in range(2)}
 
@@ -61,7 +61,7 @@ def tile_picked_triplet_none_e_kernel(tc, xT, w1_words, w1_scales, margin, offs,
                                 rhs=codes[:].bitcast(FP8X4), rhs_scale=scales[:], start=start, stop=stop)
 
         for t in range(PACK):
-            nc.vector.tensor_copy(picked_a[:, :, t], planes[t][:].indirect(entries(0, V)))
+            nc.vector.tensor_copy(picked_a[:, :, t], planes[t][:].indirect(entries(0, V + HALF)))
             for k, lo in pieces.items():
                 nc.scalar.activation(dense[k, t // 2][:, t % 2, :], planes[t][:].indirect(entries(lo, HALF)), ACT.Copy, scale=-1.0)
             if t == 1:
@@ -79,19 +79,18 @@ def tile_picked_triplet_none_e_kernel(tc, xT, w1_words, w1_scales, margin, offs,
 
         place("p1", 1, nc.scalar.copy)
         place("n1", 1, nc.scalar.copy)
-        place("p0", 1)
+        place("n0", 1)
         qa0 = quantize("a0", picked_a[:, cols(0), :], HALF)
         project(x0, qa0, True, True)
         nc.scalar.copy(anchor0[:], x0[:])
-        place("n0", 1)
-        project(y0, quantize("p0", picked["p0"][:], HALF), True, True)
+        project(y0, quantize("p0", picked_a[:, cols(2), :], HALF), True, True)
         qa1 = quantize("a1", picked_a[:, cols(1), :], HALF)
         project(z0, quantize("n0", picked["n0"][:], HALF), True, True)
         project(g1, qa1, True, False)
         project(g2, qa1, True, False)
         project(g1, quantize("p1", picked["p1"][:], HALF), False, True)
         project(g2, quantize("n1", picked["n1"][:], HALF), False, True)
-        nc.vector.tensor_tensor(d_pos0[:], y0[:], anchor0[:], ALU.add)
+        nc.vector.tensor_tensor(d_pos0[:], y0[:], anchor0[:], ALU.subtract)
         nc.vector.tensor_tensor(d_neg0[:], z0[:], anchor0[:], ALU.add)
 
         nc.scalar.activation(near[0][:], d_pos0[:], ACT.Square)

@@ -36,9 +36,9 @@ def tile_picked_triplet_none_e_kernel(tc, xT, w1_words, w1_scales, margin, offs,
             nc.sync.dma_start(planes[t][:], rows[t])
             if t == 0:
                 nc.sync.dma_start(offsets[:], offs)
-        nc.sync.dma_start(w_codes[:].bitcast(I32), w1_words[0].bitcast(I32))
+        nc.scalar.dma_start(w_codes[:].bitcast(I32), w1_words[0].bitcast(I32))
         for q in range(4):
-            nc.sync.dma_start(w_scales[32 * q : 32 * q + 4, :].bitcast(I32), w1_scales[0, 4 * q : 4 * q + 4, :].bitcast(I32))
+            nc.scalar.dma_start(w_scales[32 * q : 32 * q + 4, :].bitcast(I32), w1_scales[0, 4 * q : 4 * q + 4, :].bitcast(I32))
         nc.sync.dma_start(margins[:], margin)
 
         pieces = {"n0": 2 * V, "p1": V + HALF, "n1": 2 * V + HALF}

@@ -21,9 +21,9 @@ HALF = V // 2
 def tile_picked_triplet_none_e_kernel(tc, xT, w1_words, w1_scales, margin, offs, out):
     nc = tc.nc
     with tc.tile_pool(name="sb", bufs=1) as sb, tc.psum_pool(name="ps", bufs=1) as ps:
-        rows = xT.rearrange("(p t) c -> t p c", t=PACK)
+        rows = xT.rearrange("(p t) c -> p t c", t=PACK)
         offsets = sb.tile([P, S // 16], U16, name="offsets")
-        planes = [sb.tile([P, T], F32, name="plane%d" % t) for t in range(PACK)]
+        planes = [sb.tile([P, T], F32, name="plane%d" % t)[:] for t in range(PACK)]
         w_codes = sb.tile([P, 2 * N], U8, name="w_codes", align_bytes=64)
         w_scales = sb.tile([P, N], U8, name="w_scales", align_bytes=64)
         margins = sb.tile([P, V], F32, name="margins")
@@ -33,7 +33,7 @@ def tile_picked_triplet_none_e_kernel(tc, xT, w1_words, w1_scales, margin, offs,
 
         nc.vector.memset(w_scales[:].bitcast(I32), 0)
         for t in range(PACK):
-            nc.sync.dma_start(planes[t][:], rows[t])
+            nc.sync.dma_start(planes[t], rows[:, t, :])
             if t == 0:
                 nc.sync.dma_start(offsets[:], offs)
         nc.scalar.dma_start(w_codes[:].bitcast(I32), w1_words[0].bitcast(I32))
@@ -41,67 +41,65 @@ def tile_picked_triplet_none_e_kernel(tc, xT, w1_words, w1_scales, margin, offs,
             nc.scalar.dma_start(w_scales[32 * q : 32 * q + 4, :].bitcast(I32), w1_scales[0, 4 * q : 4 * q + 4, :].bitcast(I32))
         nc.sync.dma_start(margins[:], margin)
 
-        pieces = {"n0": 2 * V, "p1": V + HALF, "n1": 2 * V + HALF}
-        picked_a = sb.tile([P, V + HALF, PACK], BF16, name="picked_a", align_bytes=64)
+        pieces = {"n1": (2 * V + HALF, 1.0), "a0": (0, -1.0), "p0": (V, 1.0), "a1": (HALF, 1.0)}
+        picked_mid = sb.tile([P, V, PACK], BF16, name="picked_mid", align_bytes=64)
         picked = {k: sb.tile([P, HALF, PACK], BF16, name="picked_" + k, align_bytes=64) for k in pieces}
         dense = {(k, u): sb.tile([P, 2, HALF], BF16, name="dense_%s_%d" % (k, u)) for k in pieces for u in range(2)}
 
-        def place(k, u, copy=nc.vector.tensor_copy):
-            copy(picked[k][:, :, 2 * u : 2 * u + 2], dense[k, u][:].rearrange("p t n -> p n t"))
+        def place(k, u, copy=nc.vector.tensor_copy, lo=0, hi=HALF):
+            copy(picked[k][:, lo:hi, 2 * u : 2 * u + 2], dense[k, u][:, :, lo:hi].rearrange("p t n -> p n t"))
 
-        def quantize(name, source, n):
-            codes = sb.tile([P, n], U32, name="codes_" + name, align_bytes=64)
-            scales = sb.tile([P, n], U8, name="scales_" + name, align_bytes=64)
+        def quantize(name, source):
+            codes = sb.tile([P, HALF], U32, name="codes_" + name, align_bytes=64)
+            scales = sb.tile([P, HALF], U8, name="scales_" + name, align_bytes=64)
             nc.vector.quantize_mx(codes[:].bitcast(FP8X4), scales[:], source.rearrange("p n t -> p (n t)"))
             return codes, scales
 
-        def project(h, operand, start, stop):
+        def project(h, operand, start=True, stop=True):
             codes, scales = operand
             nc.tensor.matmul_mx(h[:], lhsT=w_codes[:].bitcast(FP4X4), lhsT_scale=w_scales[:],
                                 rhs=codes[:].bitcast(FP8X4), rhs_scale=scales[:], start=start, stop=stop)
 
         for t in range(PACK):
-            nc.vector.tensor_copy(picked_a[:, :, t], planes[t][:].indirect(entries(0, V + HALF)))
-            for k, lo in pieces.items():
-                nc.scalar.activation(dense[k, t // 2][:, t % 2, :], planes[t][:].indirect(entries(lo, HALF)), ACT.Copy, scale=-1.0)
+            nc.vector.tensor_copy(picked_mid[:, :, t], planes[t].indirect(entries(V + HALF, V)))
+            for k, (lo, sign) in pieces.items():
+                nc.scalar.activation(dense[k, t // 2][:, t % 2, :], planes[t].indirect(entries(lo, HALF)), ACT.Copy, scale=sign)
             if t == 1:
                 for k in pieces:
                     place(k, 0)
 
-        x0, y0, z0, g1, g2 = [ps.tile([P, HALF], F32, name=name) for name in ("x0", "y0", "z0", "g1", "g2")]
-        d_pos0, d_neg0, far0 = [sb.tile([P, HALF], F32, name=name) for name in ("d_pos0", "d_neg0", "far0")]
-        anchor0 = sb.tile([P, HALF], F32, name="anchor0", tag="anchor0")
-        near, near_m, gap, loss = [[sb.tile([P, HALF], F32, name="%s%d" % (name, j)) for j in range(2)]
-                                   for name in ("near", "near_m", "gap", "loss")]
+        h_p1, h_n1, h_a1, d_far, d_near = [ps.tile([P, HALF], F32, name=name) for name in ("h_p1", "h_n1", "h_a1", "d_far", "d_near")]
+        names = ("p_sq", "n_copy", "n_sq", "far", "near", "p_sq_m", "n_less_p", "const", "far_m", "cross", "gap0", "gap1", "loss0", "loss1")
+        p_sq, n_copy, n_sq, far, near, p_sq_m, n_less_p, const, far_m, cross, gap0, gap1, loss0, loss1 = [
+            sb.tile([P, HALF], F32, name=name) for name in names]
 
-        def cols(j):
-            return slice(j * HALF, (j + 1) * HALF)
+        place("p0", 1, nc.scalar.copy)
+        place("a1", 1, nc.scalar.copy, HALF // 2, HALF)
+        place("n1", 1)
+        project(h_p1, quantize("p1", picked_mid[:, :HALF, :]))
+        place("a0", 1)
+        project(h_n1, quantize("n1", picked["n1"][:]))
+        project(d_far, quantize("n0", picked_mid[:, HALF:, :]), True, False)
+        minus_a0 = quantize("a0", picked["a0"][:])
+        project(d_far, minus_a0, False, True)
+        project(d_near, minus_a0, True, False)
+        place("a1", 1, nc.vector.tensor_copy, 0, HALF // 2)
+        project(d_near, quantize("p0", picked["p0"][:]), False, True)
+        project(h_a1, quantize("a1", picked["a1"][:]))
 
-        place("p1", 1, nc.scalar.copy)
-        place("n1", 1, nc.scalar.copy)
-        place("n0", 1)
-        qa0 = quantize("a0", picked_a[:, cols(0), :], HALF)
-        project(x0, qa0, True, True)
-        nc.scalar.copy(anchor0[:], x0[:])
-        project(y0, quantize("p0", picked_a[:, cols(2), :], HALF), True, True)
-        qa1 = quantize("a1", picked_a[:, cols(1), :], HALF)
-        project(z0, quantize("n0", picked["n0"][:], HALF), True, True)
-        project(g1, qa1, True, False)
-        project(g2, qa1, True, False)
-        project(g1, quantize("p1", picked["p1"][:], HALF), False, True)
-        project(g2, quantize("n1", picked["n1"][:], HALF), False, True)
-        nc.vector.tensor_tensor(d_pos0[:], y0[:], anchor0[:], ALU.subtract)
-        nc.vector.tensor_tensor(d_neg0[:], z0[:], anchor0[:], ALU.add)
-
-        nc.scalar.activation(near[0][:], d_pos0[:], ACT.Square)
-        nc.scalar.activation(near[1][:], g1[:], ACT.Square)
-        nc.scalar.activation(far0[:], d_neg0[:], ACT.Square)
-        far = [far0, sb.tile([P, HALF], F32, name="far1", tag="anchor0")]
-        nc.scalar.activation(far[1][:], g2[:], ACT.Square)
-        for j in (0, 1):
-            nc.vector.tensor_tensor(near_m[j][:], near[j][:], margins[:, cols(j)], ALU.add)
-        for j in (0, 1):
-            nc.vector.tensor_tensor(gap[j][:], near_m[j][:], far[j][:], ALU.subtract)
-        for j in (0, 1):
-            nc.vector.tensor_scalar_max(loss[j][:], gap[j][:], 0.0)
-            nc.sync.dma_start(out[:, cols(j)], loss[j][:])
+        nc.scalar.activation(p_sq[:], h_p1[:], ACT.Square)
+        nc.scalar.copy(n_copy[:], h_n1[:])
+        nc.scalar.activation(n_sq[:], h_n1[:], ACT.Square)
+        nc.scalar.activation(far[:], d_far[:], ACT.Square)
+        nc.scalar.activation(near[:], d_near[:], ACT.Square)
+        nc.vector.tensor_tensor(p_sq_m[:], p_sq[:], margins[:, HALF:], ALU.add)
+        nc.vector.tensor_tensor(n_less_p[:], n_copy[:], h_p1[:], ALU.subtract)
+        nc.vector.tensor_tensor(const[:], p_sq_m[:], n_sq[:], ALU.subtract)
+        nc.vector.tensor_tensor(far_m[:], far[:], margins[:, :HALF], ALU.subtract)
+        nc.vector.scalar_tensor_tensor(cross[:], h_a1[:], 2.0, n_less_p[:], ALU.mult, ALU.mult)
+        nc.vector.tensor_tensor(gap0[:], near[:], far_m[:], ALU.subtract)
+        nc.vector.tensor_tensor(gap1[:], cross[:], const[:], ALU.add)
+        nc.vector.tensor_scalar_max(loss0[:], gap0[:], 0.0)
+        nc.sync.dma_start(out[:, :HALF], loss0[:])
+        nc.vector.tensor_scalar_max(loss1[:], gap1[:], 0.0)
+        nc.sync.dma_start(out[:, HALF:], loss1[:])

@@ -41,8 +41,8 @@ def tile_picked_triplet_none_e_kernel(tc, xT, w1_words, w1_scales, margin, offs,
             nc.scalar.dma_start(w_scales[32 * q : 32 * q + 4, :].bitcast(I32), w1_scales[0, 4 * q : 4 * q + 4, :].bitcast(I32))
         nc.sync.dma_start(margins[:], margin)
 
-        pieces = {"n1": (2 * V + HALF, 1.0), "a0": (0, -1.0), "p0": (V, 1.0), "a1": (HALF, 1.0)}
-        picked_mid = sb.tile([P, V, PACK], BF16, name="picked_mid", align_bytes=64)
+        pieces = {"a0": (0, -1.0), "p0": (V, 1.0), "a1": (HALF, 1.0)}
+        picked_mid = sb.tile([P, V + HALF, PACK], BF16, name="picked_mid", align_bytes=64)
         picked = {k: sb.tile([P, HALF, PACK], BF16, name="picked_" + k, align_bytes=64) for k in pieces}
         dense = {(k, u): sb.tile([P, 2, HALF], BF16, name="dense_%s_%d" % (k, u)) for k in pieces for u in range(2)}
 
@@ -61,7 +61,7 @@ def tile_picked_triplet_none_e_kernel(tc, xT, w1_words, w1_scales, margin, offs,
                                 rhs=codes[:].bitcast(FP8X4), rhs_scale=scales[:], start=start, stop=stop)
 
         for t in range(PACK):
-            nc.vector.tensor_copy(picked_mid[:, :, t], planes[t].indirect(entries(V + HALF, V)))
+            nc.vector.tensor_copy(picked_mid[:, :, t], planes[t].indirect(entries(V + HALF, V + HALF)))
             for k, (lo, sign) in pieces.items():
                 nc.scalar.activation(dense[k, t // 2][:, t % 2, :], planes[t].indirect(entries(lo, HALF)), ACT.Copy, scale=sign)
             if t == 1:
@@ -74,16 +74,14 @@ def tile_picked_triplet_none_e_kernel(tc, xT, w1_words, w1_scales, margin, offs,
             sb.tile([P, HALF], F32, name=name) for name in names]
 
         place("p0", 1, nc.scalar.copy)
-        place("a1", 1, nc.scalar.copy, HALF // 2, HALF)
-        place("n1", 1)
-        project(h_p1, quantize("p1", picked_mid[:, :HALF, :]))
+        place("a1", 1, nc.scalar.copy)
         place("a0", 1)
-        project(h_n1, quantize("n1", picked["n1"][:]))
-        project(d_far, quantize("n0", picked_mid[:, HALF:, :]), True, False)
+        project(h_p1, quantize("p1", picked_mid[:, :HALF, :]))
+        project(h_n1, quantize("n1", picked_mid[:, V:, :]))
+        project(d_far, quantize("n0", picked_mid[:, HALF:V, :]), True, False)
         minus_a0 = quantize("a0", picked["a0"][:])
         project(d_far, minus_a0, False, True)
         project(d_near, minus_a0, True, False)
-        place("a1", 1, nc.vector.tensor_copy, 0, HALF // 2)
         project(d_near, quantize("p0", picked["p0"][:]), False, True)
         project(h_a1, quantize("a1", picked["a1"][:]))
 

@@ -76,23 +76,27 @@ def tile_picked_triplet_none_e_kernel(tc, xT, w1_words, w1_scales, margin, offs,
         place("p0", 1, nc.scalar.copy)
         place("a1", 1, nc.scalar.copy)
         place("a0", 1)
-        project(h_p1, quantize("p1", picked_mid[:, :HALF, :]))
-        project(h_n1, quantize("n1", picked_mid[:, V:, :]))
-        project(d_far, quantize("n0", picked_mid[:, HALF:V, :]), True, False)
+        q_n1 = quantize("n1", picked_mid[:, V:, :])
+        project(h_n1, q_n1)
+        q_p1 = quantize("p1", picked_mid[:, :HALF, :])
+        project(h_p1, q_p1)
+        q_n0 = quantize("n0", picked_mid[:, HALF:V, :])
+        project(d_far, q_n0, True, False)
         minus_a0 = quantize("a0", picked["a0"][:])
         project(d_far, minus_a0, False, True)
         project(d_near, minus_a0, True, False)
-        project(d_near, quantize("p0", picked["p0"][:]), False, True)
-        project(h_a1, quantize("a1", picked["a1"][:]))
-
-        nc.scalar.activation(p_sq[:], h_p1[:], ACT.Square)
+        q_p0 = quantize("p0", picked["p0"][:])
+        project(d_near, q_p0, False, True)
+        q_a1 = quantize("a1", picked["a1"][:])
+        project(h_a1, q_a1)
         nc.scalar.copy(n_copy[:], h_n1[:])
         nc.scalar.activation(n_sq[:], h_n1[:], ACT.Square)
+        nc.scalar.activation(p_sq[:], h_p1[:], ACT.Square)
         nc.scalar.activation(far[:], d_far[:], ACT.Square)
         nc.scalar.activation(near[:], d_near[:], ACT.Square)
-        nc.vector.tensor_tensor(p_sq_m[:], p_sq[:], margins[:, HALF:], ALU.add)
+        nc.vector.tensor_tensor(p_sq_m[:], n_sq[:], margins[:, HALF:], ALU.subtract)
         nc.vector.tensor_tensor(n_less_p[:], n_copy[:], h_p1[:], ALU.subtract)
-        nc.vector.tensor_tensor(const[:], p_sq_m[:], n_sq[:], ALU.subtract)
+        nc.vector.tensor_tensor(const[:], p_sq[:], p_sq_m[:], ALU.subtract)
         nc.vector.tensor_tensor(far_m[:], far[:], margins[:, :HALF], ALU.subtract)
         nc.vector.scalar_tensor_tensor(cross[:], h_a1[:], 2.0, n_less_p[:], ALU.mult, ALU.mult)
         nc.vector.tensor_tensor(gap0[:], near[:], far_m[:], ALU.subtract)

@@ -17,6 +17,9 @@ PACK = 4
 FLOPS = 2 * K * N * S
 HALF = V // 2
 
+SPLIT_P1 = 64
+SPLIT_A1 = 64
+
 
 def tile_picked_triplet_none_e_kernel(tc, xT, w1_words, w1_scales, margin, offs, out):
     nc = tc.nc
@@ -41,12 +44,15 @@ def tile_picked_triplet_none_e_kernel(tc, xT, w1_words, w1_scales, margin, offs,
             nc.scalar.dma_start(w_scales[32 * q : 32 * q + 4, :].bitcast(I32), w1_scales[0, 4 * q : 4 * q + 4, :].bitcast(I32))
         nc.sync.dma_start(margins[:], margin)
 
-        pieces = {"a0": (0, -1.0), "p0": (V, 1.0), "a1": (HALF, 1.0)}
-        picked_mid = sb.tile([P, V + HALF, PACK], BF16, name="picked_mid", align_bytes=64)
-        picked = {k: sb.tile([P, HALF, PACK], BF16, name="picked_" + k, align_bytes=64) for k in pieces}
-        dense = {(k, u): sb.tile([P, 2, HALF], BF16, name="dense_%s_%d" % (k, u)) for k in pieces for u in range(2)}
+        upper = V + HALF
+        pieces = {"p1": (upper, SPLIT_P1, 1.0), "a0": (0, HALF, -1.0), "p0": (V, HALF, 1.0), "a1": (HALF, HALF, 1.0)}
+        picked_mid = sb.tile([P, S - upper, PACK], BF16, name="picked_mid", align_bytes=64)
+        picked = {k: sb.tile([P, HALF, PACK], BF16, name="picked_" + k, align_bytes=64) for k in ("a0", "p0", "a1")}
+        picked["p1"] = picked_mid
+        dense = {(k, u): sb.tile([P, 2, pieces[k][1]], BF16, name="dense_%s_%d" % (k, u)) for k in pieces for u in range(2)}
 
-        def place(k, u, copy=nc.vector.tensor_copy, lo=0, hi=HALF):
+        def place(k, u, copy=nc.vector.tensor_copy, lo=0, hi=None):
+            hi = pieces[k][1] if hi is None else hi
             copy(picked[k][:, lo:hi, 2 * u : 2 * u + 2], dense[k, u][:, :, lo:hi].rearrange("p t n -> p n t"))
 
         def quantize(name, source):
@@ -61,9 +67,9 @@ def tile_picked_triplet_none_e_kernel(tc, xT, w1_words, w1_scales, margin, offs,
                                 rhs=codes[:].bitcast(FP8X4), rhs_scale=scales[:], start=start, stop=stop)
 
         for t in range(PACK):
-            nc.vector.tensor_copy(picked_mid[:, :, t], planes[t].indirect(entries(V + HALF, V + HALF)))
-            for k, (lo, sign) in pieces.items():
-                nc.scalar.activation(dense[k, t // 2][:, t % 2, :], planes[t].indirect(entries(lo, HALF)), ACT.Copy, scale=sign)
+            nc.vector.tensor_copy(picked_mid[:, SPLIT_P1:, t], planes[t].indirect(entries(upper + SPLIT_P1, S - upper - SPLIT_P1)))
+            for k, (lo, n, sign) in pieces.items():
+                nc.scalar.activation(dense[k, t // 2][:, t % 2, :], planes[t].indirect(entries(lo, n)), ACT.Copy, scale=sign)
             if t == 1:
                 for k in pieces:
                     place(k, 0)
@@ -74,7 +80,8 @@ def tile_picked_triplet_none_e_kernel(tc, xT, w1_words, w1_scales, margin, offs,
             sb.tile([P, HALF], F32, name=name) for name in names]
 
         place("p0", 1, nc.scalar.copy)
-        place("a1", 1, nc.scalar.copy)
+        place("a1", 1, nc.scalar.copy, SPLIT_A1, HALF)
+        place("p1", 1)
         place("a0", 1)
         q_n1 = quantize("n1", picked_mid[:, V:, :])
         project(h_n1, q_n1)
@@ -85,23 +92,31 @@ def tile_picked_triplet_none_e_kernel(tc, xT, w1_words, w1_scales, margin, offs,
         minus_a0 = quantize("a0", picked["a0"][:])
         project(d_far, minus_a0, False, True)
         project(d_near, minus_a0, True, False)
+        place("a1", 1, nc.vector.tensor_copy, 0, SPLIT_A1)
         q_p0 = quantize("p0", picked["p0"][:])
         project(d_near, q_p0, False, True)
         q_a1 = quantize("a1", picked["a1"][:])
         project(h_a1, q_a1)
+        quarters = [slice(0, HALF // 2), slice(HALF // 2, HALF)]
         nc.scalar.copy(n_copy[:], h_n1[:])
         nc.scalar.activation(n_sq[:], h_n1[:], ACT.Square)
         nc.scalar.activation(p_sq[:], h_p1[:], ACT.Square)
         nc.scalar.activation(far[:], d_far[:], ACT.Square)
         nc.scalar.activation(near[:], d_near[:], ACT.Square)
         nc.vector.tensor_tensor(p_sq_m[:], n_sq[:], margins[:, HALF:], ALU.subtract)
-        nc.vector.tensor_tensor(n_less_p[:], n_copy[:], h_p1[:], ALU.subtract)
+        for c in quarters:
+            nc.vector.tensor_tensor(n_less_p[:, c], n_copy[:, c], h_p1[:, c], ALU.subtract)
         nc.vector.tensor_tensor(const[:], p_sq[:], p_sq_m[:], ALU.subtract)
         nc.vector.tensor_tensor(far_m[:], far[:], margins[:, :HALF], ALU.subtract)
-        nc.vector.scalar_tensor_tensor(cross[:], h_a1[:], 2.0, n_less_p[:], ALU.mult, ALU.mult)
-        nc.vector.tensor_tensor(gap0[:], near[:], far_m[:], ALU.subtract)
-        nc.vector.tensor_tensor(gap1[:], cross[:], const[:], ALU.add)
-        nc.vector.tensor_scalar_max(loss0[:], gap0[:], 0.0)
+        for c in quarters:
+            nc.vector.scalar_tensor_tensor(cross[:, c], h_a1[:, c], 2.0, n_less_p[:, c], ALU.mult, ALU.mult)
+        for c in quarters:
+            nc.vector.tensor_tensor(gap0[:, c], near[:, c], far_m[:, c], ALU.subtract)
+        for c in quarters:
+            nc.vector.tensor_tensor(gap1[:, c], cross[:, c], const[:, c], ALU.add)
+        for c in quarters:
+            nc.vector.tensor_scalar_max(loss0[:, c], gap0[:, c], 0.0)
         nc.sync.dma_start(out[:, :HALF], loss0[:])
-        nc.vector.tensor_scalar_max(loss1[:], gap1[:], 0.0)
+        for c in quarters:
+            nc.vector.tensor_scalar_max(loss1[:, c], gap1[:, c], 0.0)
         nc.sync.dma_start(out[:, HALF:], loss1[:])

@@ -23,7 +23,7 @@ SPLIT_A1 = 64
 
 def tile_picked_triplet_none_e_kernel(tc, xT, w1_words, w1_scales, margin, offs, out):
     nc = tc.nc
-    with tc.tile_pool(name="sb", bufs=1) as sb, tc.psum_pool(name="ps", bufs=1) as ps:
+    with tc.tile_pool(name="sb", bufs=1) as sb, tc.tile_pool(name="shared", bufs=1) as shared, tc.psum_pool(name="ps", bufs=1) as ps:
         rows = xT.rearrange("(p t) c -> p t c", t=PACK)
         offsets = sb.tile([P, S // 16], U16, name="offsets")
         planes = [sb.tile([P, T], F32, name="plane%d" % t)[:] for t in range(PACK)]
@@ -49,7 +49,8 @@ def tile_picked_triplet_none_e_kernel(tc, xT, w1_words, w1_scales, margin, offs,
         picked_mid = sb.tile([P, S - upper, PACK], BF16, name="picked_mid", align_bytes=64)
         picked = {k: sb.tile([P, HALF, PACK], BF16, name="picked_" + k, align_bytes=64) for k in ("a0", "p0", "a1")}
         picked["p1"] = picked_mid
-        dense = {(k, u): sb.tile([P, 2, pieces[k][1]], BF16, name="dense_%s_%d" % (k, u)) for k in pieces for u in range(2)}
+        dense = {(k, u): sb.tile([P, 2, pieces[k][1]], BF16, name="dense_%s_%d" % (k, u)) for k in pieces for u in range(2) if (k, u) != ("p1", 1)}
+        dense["p1", 1] = shared.tile([P, 2, SPLIT_P1], BF16, name="dense_p1_1", offset=0, align_bytes=64)
 
         def place(k, u, copy=nc.vector.tensor_copy, lo=0, hi=None):
             hi = pieces[k][1] if hi is None else hi
@@ -57,7 +58,10 @@ def tile_picked_triplet_none_e_kernel(tc, xT, w1_words, w1_scales, margin, offs,
 
         def quantize(name, source):
             codes = sb.tile([P, HALF], U32, name="codes_" + name, align_bytes=64)
-            scales = sb.tile([P, HALF], U8, name="scales_" + name, align_bytes=64)
+            if name in ("n0", "n1"):
+                scales = shared.tile([P, HALF], U8, name="scales_" + name, offset=HALF * int(name[1]), align_bytes=64)
+            else:
+                scales = sb.tile([P, HALF], U8, name="scales_" + name, align_bytes=64)
             nc.vector.quantize_mx(codes[:].bitcast(FP8X4), scales[:], source.rearrange("p n t -> p (n t)"))
             return codes, scales
 

@@ -17,7 +17,7 @@ PACK = 4
 FLOPS = 2 * K * N * S
 HALF = V // 2
 
-SPLIT_P1 = 64
+SPLIT_P1 = 96
 SPLIT_A1 = 64
 
 

@@ -17,7 +17,7 @@ PACK = 4
 FLOPS = 2 * K * N * S
 HALF = V // 2
 
-SPLIT_P1 = 96
+SPLIT_P1 = 128
 SPLIT_A1 = 64
 
 

@@ -17,7 +17,6 @@ PACK = 4
 FLOPS = 2 * K * N * S
 HALF = V // 2
 
-SPLIT_P1 = 128
 SPLIT_A1 = 64
 
 
@@ -45,12 +44,11 @@ def tile_picked_triplet_none_e_kernel(tc, xT, w1_words, w1_scales, margin, offs,
         nc.sync.dma_start(margins[:], margin)
 
         upper = V + HALF
-        pieces = {"p1": (upper, SPLIT_P1, 1.0), "a0": (0, HALF, -1.0), "p0": (V, HALF, 1.0), "a1": (HALF, HALF, 1.0)}
+        pieces = {"a0": (0, HALF, -1.0), "p0": (V, HALF, 1.0), "a1": (HALF, HALF, 1.0)}
         picked_mid = sb.tile([P, S - upper, PACK], BF16, name="picked_mid", align_bytes=64)
-        picked = {k: sb.tile([P, HALF, PACK], BF16, name="picked_" + k, align_bytes=64) for k in ("a0", "p0", "a1")}
-        picked["p1"] = picked_mid
-        dense = {(k, u): sb.tile([P, 2, pieces[k][1]], BF16, name="dense_%s_%d" % (k, u)) for k in pieces for u in range(2) if (k, u) != ("p1", 1)}
-        dense["p1", 1] = shared.tile([P, 2, SPLIT_P1], BF16, name="dense_p1_1", offset=0, align_bytes=64)
+        picked = {k: sb.tile([P, HALF, PACK], BF16, name="picked_" + k, tag="picked_" + k, align_bytes=64) for k in ("a0", "p0", "a1")}
+        dense = {(k, u): sb.tile([P, 2, pieces[k][1]], BF16, name="dense_%s_%d" % (k, u)) for k in pieces for u in range(2)}
+        last_p1 = shared.tile([P, HALF], BF16, name="last_p1", offset=0, align_bytes=64)
 
         def place(k, u, copy=nc.vector.tensor_copy, lo=0, hi=None):
             hi = pieces[k][1] if hi is None else hi
@@ -71,22 +69,28 @@ def tile_picked_triplet_none_e_kernel(tc, xT, w1_words, w1_scales, margin, offs,
                                 rhs=codes[:].bitcast(FP8X4), rhs_scale=scales[:], start=start, stop=stop)
 
         for t in range(PACK):
-            nc.vector.tensor_copy(picked_mid[:, SPLIT_P1:, t], planes[t].indirect(entries(upper + SPLIT_P1, S - upper - SPLIT_P1)))
+            if t < PACK - 1:
+                nc.vector.tensor_copy(picked_mid[:, :, t], planes[t].indirect(entries(upper, S - upper)))
+            else:
+                nc.vector.tensor_copy(picked_mid[:, HALF:, t], planes[t].indirect(entries(2 * V, V)))
+                nc.scalar.activation(last_p1[:], planes[t].indirect(entries(upper, HALF)), ACT.Copy)
             for k, (lo, n, sign) in pieces.items():
                 nc.scalar.activation(dense[k, t // 2][:, t % 2, :], planes[t].indirect(entries(lo, n)), ACT.Copy, scale=sign)
             if t == 1:
                 for k in pieces:
                     place(k, 0)
+            if t == 2:
+                nc.vector.tensor_copy(picked["a0"][:, :, 2], dense["a0", 1][:, 0, :])
 
         h_p1, h_n1, h_a1, d_far, d_near = [ps.tile([P, HALF], F32, name=name) for name in ("h_p1", "h_n1", "h_a1", "d_far", "d_near")]
-        names = ("p_sq", "n_copy", "n_sq", "far", "near", "p_sq_m", "n_less_p", "const", "far_m", "cross", "gap0", "gap1", "loss0", "loss1")
-        p_sq, n_copy, n_sq, far, near, p_sq_m, n_less_p, const, far_m, cross, gap0, gap1, loss0, loss1 = [
+        names = ("p_sq", "p_copy", "n_sq", "far", "near", "n_less_p", "const", "far_m", "cross", "gap0", "gap1", "loss0", "loss1")
+        p_sq, p_copy, n_sq, far, near, n_less_p, const, far_m, cross, gap0, gap1, loss0, loss1 = [
             sb.tile([P, HALF], F32, name=name) for name in names]
 
         place("p0", 1, nc.scalar.copy)
         place("a1", 1, nc.scalar.copy, SPLIT_A1, HALF)
-        place("p1", 1)
-        place("a0", 1)
+        nc.vector.tensor_copy(picked_mid[:, :HALF, 3], last_p1[:])
+        nc.vector.tensor_copy(picked["a0"][:, :, 3], dense["a0", 1][:, 1, :])
         q_n1 = quantize("n1", picked_mid[:, V:, :])
         project(h_n1, q_n1)
         q_p1 = quantize("p1", picked_mid[:, :HALF, :])
@@ -102,14 +106,15 @@ def tile_picked_triplet_none_e_kernel(tc, xT, w1_words, w1_scales, margin, offs,
         q_a1 = quantize("a1", picked["a1"][:])
         project(h_a1, q_a1)
         quarters = [slice(0, HALF // 2), slice(HALF // 2, HALF)]
-        nc.scalar.copy(n_copy[:], h_n1[:])
         nc.scalar.activation(n_sq[:], h_n1[:], ACT.Square)
+        nc.scalar.copy(p_copy[:], h_p1[:])
         nc.scalar.activation(p_sq[:], h_p1[:], ACT.Square)
         nc.scalar.activation(far[:], d_far[:], ACT.Square)
         nc.scalar.activation(near[:], d_near[:], ACT.Square)
+        p_sq_m = sb.tile([P, HALF], F32, name="p_sq_m", tag="picked_p0", align_bytes=64)
         nc.vector.tensor_tensor(p_sq_m[:], n_sq[:], margins[:, HALF:], ALU.subtract)
         for c in quarters:
-            nc.vector.tensor_tensor(n_less_p[:, c], n_copy[:, c], h_p1[:, c], ALU.subtract)
+            nc.vector.tensor_tensor(n_less_p[:, c], h_n1[:, c], p_copy[:, c], ALU.subtract)
         nc.vector.tensor_tensor(const[:], p_sq[:], p_sq_m[:], ALU.subtract)
         nc.vector.tensor_tensor(far_m[:], far[:], margins[:, :HALF], ALU.subtract)
         for c in quarters:

import concourse.mybir as mybir

F32 = mybir.dt.float32
BF16 = mybir.dt.bfloat16
I32 = mybir.dt.int32
U32 = mybir.dt.uint32
U16 = mybir.dt.uint16
U8 = mybir.dt.uint8
FP8X4 = mybir.dt.float8_e4m3fn_x4
FP4X4 = mybir.dt.float4_e2m1fn_x4
ALU = mybir.AluOpType
ACT = mybir.ActivationFunctionType

K, T, S, V, N = 512, 2048, 768, 256, 128
P = 128
PACK = 4
FLOPS = 2 * K * N * S
HALF = V // 2

SPLIT_A1 = 64


def tile_picked_triplet_none_e_kernel(tc, xT, w1_words, w1_scales, margin, offs, out):
    nc = tc.nc
    with tc.tile_pool(name="sb", bufs=1) as sb, tc.tile_pool(name="shared", bufs=1) as shared, tc.psum_pool(name="ps", bufs=1) as ps:
        rows = xT.rearrange("(p t) c -> p t c", t=PACK)
        offsets = sb.tile([P, S // 16], U16, name="offsets")
        planes = [sb.tile([P, T], F32, name="plane%d" % t)[:] for t in range(PACK)]
        w_codes = sb.tile([P, 2 * N], U8, name="w_codes", align_bytes=64)
        w_scales = sb.tile([P, N], U8, name="w_scales", align_bytes=64)
        margins = sb.tile([P, V], F32, name="margins")

        def entries(lo, n):
            return offsets[:, lo // 16 : (lo + n) // 16]

        nc.vector.memset(w_scales[:].bitcast(I32), 0)
        for t in range(PACK):
            nc.sync.dma_start(planes[t], rows[:, t, :])
            if t == 0:
                nc.sync.dma_start(offsets[:], offs)
        nc.scalar.dma_start(w_codes[:].bitcast(I32), w1_words[0].bitcast(I32))
        for q in range(4):
            nc.scalar.dma_start(w_scales[32 * q : 32 * q + 4, :].bitcast(I32), w1_scales[0, 4 * q : 4 * q + 4, :].bitcast(I32))
        nc.sync.dma_start(margins[:], margin)

        upper = V + HALF
        pieces = {"a0": (0, HALF, -1.0), "p0": (V, HALF, 1.0), "a1": (HALF, HALF, 1.0)}
        picked_mid = sb.tile([P, S - upper, PACK], BF16, name="picked_mid", align_bytes=64)
        picked = {k: sb.tile([P, HALF, PACK], BF16, name="picked_" + k, tag="picked_" + k, align_bytes=64) for k in ("a0", "p0", "a1")}
        dense = {(k, u): sb.tile([P, 2, pieces[k][1]], BF16, name="dense_%s_%d" % (k, u)) for k in pieces for u in range(2)}
        last_p1 = shared.tile([P, HALF], BF16, name="last_p1", offset=0, align_bytes=64)

        def place(k, u, copy=nc.vector.tensor_copy, lo=0, hi=None):
            hi = pieces[k][1] if hi is None else hi
            copy(picked[k][:, lo:hi, 2 * u : 2 * u + 2], dense[k, u][:, :, lo:hi].rearrange("p t n -> p n t"))

        def quantize(name, source):
            codes = sb.tile([P, HALF], U32, name="codes_" + name, align_bytes=64)
            if name in ("n0", "n1"):
                scales = shared.tile([P, HALF], U8, name="scales_" + name, offset=HALF * int(name[1]), align_bytes=64)
            else:
                scales = sb.tile([P, HALF], U8, name="scales_" + name, align_bytes=64)
            nc.vector.quantize_mx(codes[:].bitcast(FP8X4), scales[:], source.rearrange("p n t -> p (n t)"))
            return codes, scales

        def project(h, operand, start=True, stop=True):
            codes, scales = operand
            nc.tensor.matmul_mx(h[:], lhsT=w_codes[:].bitcast(FP4X4), lhsT_scale=w_scales[:],
                                rhs=codes[:].bitcast(FP8X4), rhs_scale=scales[:], start=start, stop=stop)

        for t in range(PACK):
            if t < PACK - 1:
                nc.vector.tensor_copy(picked_mid[:, :, t], planes[t].indirect(entries(upper, S - upper)))
            else:
                nc.vector.tensor_copy(picked_mid[:, HALF:, t], planes[t].indirect(entries(2 * V, V)))
                nc.scalar.activation(last_p1[:], planes[t].indirect(entries(upper, HALF)), ACT.Copy)
            for k, (lo, n, sign) in pieces.items():
                nc.scalar.activation(dense[k, t // 2][:, t % 2, :], planes[t].indirect(entries(lo, n)), ACT.Copy, scale=sign)
            if t == 1:
                for k in pieces:
                    place(k, 0)
            if t == 2:
                nc.vector.tensor_copy(picked["a0"][:, :, 2], dense["a0", 1][:, 0, :])

        h_p1, h_n1, h_a1, d_far, d_near = [ps.tile([P, HALF], F32, name=name) for name in ("h_p1", "h_n1", "h_a1", "d_far", "d_near")]
        names = ("p_sq", "p_copy", "n_sq", "far", "near", "n_less_p", "const", "far_m", "cross", "gap0", "gap1", "loss0", "loss1")
        p_sq, p_copy, n_sq, far, near, n_less_p, const, far_m, cross, gap0, gap1, loss0, loss1 = [
            sb.tile([P, HALF], F32, name=name) for name in names]

        place("p0", 1, nc.scalar.copy)
        place("a1", 1, nc.scalar.copy, SPLIT_A1, HALF)
        nc.vector.tensor_copy(picked_mid[:, :HALF, 3], last_p1[:])
        nc.vector.tensor_copy(picked["a0"][:, :, 3], dense["a0", 1][:, 1, :])
        q_n1 = quantize("n1", picked_mid[:, V:, :])
        project(h_n1, q_n1)
        q_p1 = quantize("p1", picked_mid[:, :HALF, :])
        project(h_p1, q_p1)
        q_n0 = quantize("n0", picked_mid[:, HALF:V, :])
        project(d_far, q_n0, True, False)
        minus_a0 = quantize("a0", picked["a0"][:])
        project(d_far, minus_a0, False, True)
        project(d_near, minus_a0, True, False)
        place("a1", 1, nc.vector.tensor_copy, 0, SPLIT_A1)
        q_p0 = quantize("p0", picked["p0"][:])
        project(d_near, q_p0, False, True)
        q_a1 = quantize("a1", picked["a1"][:])
        project(h_a1, q_a1)
        quarters = [slice(0, HALF // 2), slice(HALF // 2, HALF)]
        nc.scalar.activation(n_sq[:], h_n1[:], ACT.Square)
        nc.scalar.copy(p_copy[:], h_p1[:])
        nc.scalar.activation(p_sq[:], h_p1[:], ACT.Square)
        nc.scalar.activation(far[:], d_far[:], ACT.Square)
        nc.scalar.activation(near[:], d_near[:], ACT.Square)
        p_sq_m = sb.tile([P, HALF], F32, name="p_sq_m", tag="picked_p0", align_bytes=64)
        nc.vector.tensor_tensor(p_sq_m[:], n_sq[:], margins[:, HALF:], ALU.subtract)
        for c in quarters:
            nc.vector.tensor_tensor(n_less_p[:, c], h_n1[:, c], p_copy[:, c], ALU.subtract)
        nc.vector.tensor_tensor(const[:], p_sq[:], p_sq_m[:], ALU.subtract)
        nc.vector.tensor_tensor(far_m[:], far[:], margins[:, :HALF], ALU.subtract)
        for c in quarters:
            nc.vector.scalar_tensor_tensor(cross[:, c], h_a1[:, c], 2.0, n_less_p[:, c], ALU.mult, ALU.mult)
        for c in quarters:
            nc.vector.tensor_tensor(gap0[:, c], near[:, c], far_m[:, c], ALU.subtract)
        for c in quarters:
            nc.vector.tensor_tensor(gap1[:, c], cross[:, c], const[:, c], ALU.add)
        for c in quarters:
            nc.vector.tensor_scalar_max(loss0[:, c], gap0[:, c], 0.0)
        nc.sync.dma_start(out[:, :HALF], loss0[:])
        for c in quarters:
            nc.vector.tensor_scalar_max(loss1[:, c], gap1[:, c], 0.0)
        nc.sync.dma_start(out[:, HALF:], loss1[:])
